import numpy as np
import ml_dtypes


def mxq(x, axis, fmt="e4m3"):
    dtype, down = {"e4m3": (ml_dtypes.float8_e4m3fn, 7), "e5m2": (ml_dtypes.float8_e5m2, 14)}[fmt]
    v = np.moveaxis(np.asarray(x, np.float32).astype(ml_dtypes.bfloat16).astype(np.float64), axis, -1)
    blocks = v.reshape(v.shape[:-1] + (-1, 32))
    amax = np.abs(blocks).max(-1, keepdims=True)
    byte = np.maximum(np.where(amax > 0, np.frexp(amax)[1] - 1 + 127, 0) - down, 1)
    scale = np.exp2(byte - 127.0)
    codes = (blocks / scale).astype(np.float32).astype(dtype).astype(np.float64)
    return np.moveaxis((codes * scale).reshape(v.shape), -1, axis)


WIDE = False


def mx_kscale(k):
    if not WIDE:
        return np.ones(k)
    levels = np.array([10, -10, 5, -5, 0])
    if k % 512:
        return np.exp2(np.random.permutation(np.resize(levels, k // 32))).repeat(32)
    a = np.empty((k // 512, 16))
    for p in range(k // 512):
        a[p, :8] = np.random.permutation(np.resize(levels, 8))
        for g in range(8):
            far = levels[np.abs(levels - a[p, g]) >= 10]
            a[p, g + 8] = far[np.random.randint(len(far))]
    return np.exp2(a.ravel()).repeat(32)


def f64(x):
    return np.asarray(x).astype(np.float64)


def striped(idx):
    return np.tile(idx.reshape(-1, 16).T, (8, 1)).astype(np.uint16)


def unstriped(offs):
    return offs[:16].T.reshape(-1).astype(np.int64)


E2M1 = np.array([0.0, 0.5, 1.0, 1.5, 2.0, 3.0, 4.0, 6.0, -0.0, -0.5, -1.0, -1.5, -2.0, -3.0, -4.0, -6.0])


def pack_weight(w, fmt):
    k, n = w.shape
    w = f64(np.asarray(w, np.float32).astype(ml_dtypes.bfloat16)).reshape(k // 32, 32, n)
    amax = np.abs(w).max(1)
    if fmt == "e4m3":
        byte = np.frexp(amax)[1] - 1 + 127 - 7
    else:
        mant, ex = np.frexp(amax / 6.0)
        byte = np.where(mant > 0.5, ex, ex - 1) + 127
    byte = np.clip(np.where(amax > 0, byte, 1), 1, 254)
    scaled = (w * np.exp2(127.0 - byte)[:, None, :]).reshape(k, n).astype(np.float32)
    by_word = np.ascontiguousarray(scaled.reshape(k // 512, 128, 4, n).transpose(0, 1, 3, 2))
    if fmt == "e4m3":
        words = by_word.astype(ml_dtypes.float8_e4m3fn).view(np.uint8)
    else:
        c = by_word.astype(ml_dtypes.float4_e2m1fn).view(np.uint8) & 0xF
        words = (c[..., 0::2] | (c[..., 1::2] << 4)).reshape(k // 512, 128, 2 * n)
    return np.ascontiguousarray(words), np.ascontiguousarray(byte.astype(np.uint8).reshape(k // 512, 16, n))


def unpack_weight(words, scales, fmt):
    g, _, n = scales.shape
    words = np.ascontiguousarray(words).reshape(g, 128, n, -1)
    if fmt == "e4m3":
        vals = words.view(ml_dtypes.float8_e4m3fn).astype(np.float64)
    else:
        nib = np.empty((g, 128, n, 4), np.uint8)
        nib[..., 0::2] = words & 0xF
        nib[..., 1::2] = words >> 4
        vals = E2M1[nib]
    vals = vals * np.repeat(np.exp2(scales.astype(np.float64) - 127.0), 8, axis=1)[..., None]
    return vals.transpose(0, 1, 3, 2).reshape(g * 512, n)


def gelu(v):
    return 0.5 * v * (1.0 + np.tanh(np.sqrt(2.0 / np.pi) * (v + 0.044715 * v**3)))


def bf(x):
    return np.asarray(x, np.float32).astype(ml_dtypes.bfloat16)


def planes(Y):
    n, m = Y.shape
    b = f64(bf(Y)).reshape(n // 32, 32, m)
    amax = np.abs(b).max(1)
    byte = np.clip(np.where(amax > 0, np.frexp(amax)[1] - 1 + 127 - 7, 1), 1, 254)
    codes = (b * np.exp2(127.0 - byte)[:, None, :]).reshape(n, m).astype(np.float32).astype(ml_dtypes.float8_e4m3fn).view(np.uint8)
    words = codes.reshape(n // 512, 128, 4, m).transpose(0, 1, 3, 2)
    return np.ascontiguousarray(words), np.ascontiguousarray(byte.astype(np.uint8).reshape(n // 512, 16, m))


K, H, N, T, S, P = 1024, 1024, 512, 2048, 1024, 512

def setup_inputs():
    n = np.random.standard_normal
    s = mx_kscale(K)[:, None]
    u = mx_kscale(H)[:, None]
    tab_words, tab_scales = pack_weight(n((K, T)) * s, "e4m3")
    w1_words, w1_scales = pack_weight(n((K, H)) / np.sqrt(K) / s * u.T, "e2m1")
    wd_words, wd_scales = pack_weight(n((H, N)) / np.sqrt(H) / u, "e4m3")
    return {
        "tab_words": tab_words, "tab_scales": tab_scales,
        "offs": striped(np.random.permutation(T)[:S]),
        "pos1": striped(np.random.permutation(S)[:P]),
        "pos2": striped(np.random.permutation(S)[:P]),
        "w1_words": w1_words, "w1_scales": w1_scales,
        "least": ((0.5 * n(H) - 0.5) * u[:, 0]).astype(np.float32),
        "wr": (n((H, N)) / np.sqrt(H) / u).astype(np.float32),
        "wd_words": wd_words, "wd_scales": wd_scales,
        "base": np.random.uniform(0.05, 0.3, N).astype(np.float32),
        "gain": (3.0 * np.sign(n(N)) * np.exp(0.8 * n(N))).astype(np.float32),
    }

def reference(tab_words, tab_scales, offs, pos1, pos2, w1_words, w1_scales, least, wr, wd_words, wd_scales, base, gain):
    v = unpack_weight(tab_words, tab_scales, "e4m3")[:, unstriped(offs)]
    w1 = unpack_weight(w1_words, w1_scales, "e2m1")
    wd = unpack_weight(wd_words, wd_scales, "e4m3")
    h = np.maximum(w1.T @ v, f64(least)[:, None])
    hq = mxq(h, 0, "e4m3")
    e = mxq(f64(wr), 0, "e4m3").T @ hq
    d = wd.T @ hq
    top = e.max(axis=1)
    a = np.exp(e[:, unstriped(pos1)] - top[:, None])
    c = d[:, unstriped(pos2)]
    y = f64(gain)[:, None] * ((a + f64(base)[:, None]) * c)
    words, scales = planes(y)
    return y, words, scales

@@ -1,0 +1,239 @@
+from contextlib import ExitStack
+
+import concourse.mybir as mybir
+
+K, H, N, T, S, M = 1024, 1024, 512, 2048, 1024, 512
+FLOPS = 2 * K * H * S + 4 * H * N * S
+
+F32 = mybir.dt.float32
+BF16 = mybir.dt.bfloat16
+I32 = mybir.dt.int32
+U32 = mybir.dt.uint32
+U16 = mybir.dt.uint16
+U8 = mybir.dt.uint8
+FP8X4 = mybir.dt.float8_e4m3fn_x4
+FP4X4 = mybir.dt.float4_e2m1fn_x4
+ALU = mybir.AluOpType
+ACT = mybir.ActivationFunctionType
+
+P = 128
+PACK = 4
+PASSES = 2
+GROUP = P * PACK
+UNIT = 128
+CHUNKS = ((0, 512), (512, 768), (768, 1024))
+FIRST = 256
+SHIFT_ROWS = 112
+
+
+def tile_list_reserve_activation_scores_kernel(
+    tc, tab_words, tab_scales, offs, pos1, pos2, w1_words, w1_scales, least, wr, wd_words, wd_scales, base, gain,
+    out_0, out_1, out_2,
+):
+    nc = tc.nc
+    with ExitStack() as ctx:
+        keep = ctx.enter_context(tc.tile_pool(name="keep", bufs=1))
+        h_psum = ctx.enter_context(tc.psum_pool(name="h_psum", bufs=4))
+        s_psum = ctx.enter_context(tc.psum_pool(name="s_psum", bufs=4))
+
+        def new(name, shape, dtype, tag=None):
+            return keep.tile(shape, dtype, name=name, tag=tag or name, align_bytes=64)
+
+        offs_sb = new("offs_sb", [P, S // 16], U16)
+        pos1_sb = new("pos1_sb", [P, M // 16], U16)
+        pos2_sb = new("pos2_sb", [P, M // 16], U16)
+        tab_w = [new("tab_w%d" % a, [P, T], I32) for a in range(PASSES)]
+        tab_s = new("tab_s", [P, T], U8)
+        v_w = [new("v_w%d" % a, [P, S], U32) for a in range(PASSES)]
+        v_s_all = new("v_s_all", [P, S], U8)
+        v_s = [new("v_s%d" % a, [P, S], U8) for a in range(PASSES)]
+        w1_raw = new("w1_raw", [P, PASSES, 2 * H], U8)
+        w1_w = [[new("w1_w%d%d" % (a, b), [P, 2 * GROUP], U8) for b in range(2)] for a in range(PASSES)]
+        w1_s_raw = new("w1_s_raw", [P, H], U8)
+        w1_s = [new("w1_s%d" % a, [P, H], U8) for a in range(PASSES)]
+        wd_w = new("wd_w", [P, PASSES, N], U32)
+        wd_s = new("wd_s", [P, N], U8)
+        wr_bf = [new("wr_bf%d" % b, [P, PACK * N], BF16) for b in range(2)]
+        wr_w = [new("wr_w%d" % b, [P, N], U32) for b in range(2)]
+        wr_s = [new("wr_s%d" % b, [P, N], U8) for b in range(2)]
+        least_sb = new("least_sb", [P, 2, PACK], F32)
+        base_sb = new("base_sb", [P, PACK], F32)
+        gain_sb = new("gain_sb", [P, PACK], F32)
+        gain_base = new("gain_base", [P, PACK], F32)
+        h_bf = [new("h_bf%d" % b, [P, PACK * S], BF16) for b in range(2)]
+        h_w = [new("h_w%d" % b, [P, S], U32) for b in range(2)]
+        h_s = [new("h_s%d" % b, [P, S], U8) for b in range(2)]
+        e_sb = [new("e_sb%d" % t, [P, S], F32) for t in range(PACK)]
+        d_sb = [new("d_sb%d" % t, [P, S], F32) for t in range(PACK)]
+        tops = [[new("top%d_%d" % (t, c), [P, 1], F32) for c in range(len(CHUNKS))] for t in range(PACK)]
+        neg_top = [new("neg_top%d" % t, [P, 1], F32) for t in range(PACK)]
+        a_sb = [new("a_sb%d" % t, [P, M], F32) for t in range(PACK)]
+        lift = [new("lift%d" % t, [P, M], F32) for t in range(PACK)]
+        y_sb = new("y_sb", [P, PACK, M], F32)
+        y_bf = new("y_bf", [P, PACK * M], BF16)
+        y_w = new("y_w", [P, M], U32)
+        y_s = new("y_s", [P, M], U8)
+
+        def load_scale_rows(engine, dst, src, row=0):
+            for q in range(4):
+                engine.dma_start(out=dst[32 * q + row : 32 * q + row + 8, :].bitcast(I32), in_=src[:, 4 * q : 4 * q + 4, :].bitcast(I32))
+
+        def deal(engine_copy, dst, src):
+            engine_copy(out=dst.rearrange("p (g i m) -> p g m i", i=PACK, m=P), in_=src.rearrange("p (g m i) -> p g m i", i=PACK, m=P))
+
+        nc.gpsimd.memset(w1_s_raw[:].bitcast(I32), 0)
+        for q in range(4):
+            engine = nc.vector if q < 2 else nc.gpsimd
+            engine.memset(tab_s[32 * q : 32 * q + 24, :].bitcast(I32), 0)
+        for plane in (v_s[0], v_s[1], w1_s[1]):
+            nc.gpsimd.memset(plane[:].bitcast(I32), 0)
+
+        nc.sync.dma_start(offs_sb[:], offs)
+        load_scale_rows(nc.sync, tab_s, tab_scales, 24)
+        nc.sync.dma_start(out=tab_w[0][:], in_=tab_words[0].rearrange("p t i -> p (t i)").bitcast(I32))
+        nc.sync.dma_start(out=w1_raw[:].bitcast(I32), in_=w1_words.rearrange("a p c -> p a c").bitcast(I32))
+        nc.sync.dma_start(pos1_sb[:], pos1)
+        nc.sync.dma_start(pos2_sb[:], pos2)
+        load_scale_rows(nc.scalar, w1_s_raw, w1_scales)
+        nc.sync.dma_start(out=tab_w[1][:], in_=tab_words[1].rearrange("p t i -> p (t i)").bitcast(I32))
+        nc.gpsimd.dma_start(out=least_sb[:], in_=least.rearrange("(b p i) -> p b i", b=2, i=PACK))
+        nc.gpsimd.dma_start(out=base_sb[:], in_=base.rearrange("(p t) -> p t", t=PACK))
+        nc.gpsimd.dma_start(out=gain_sb[:], in_=gain.rearrange("(p t) -> p t", t=PACK))
+
+        nc.vector.tensor_copy(out=v_s_all[:], in_=tab_s[:].indirect(offs_sb[:]))
+        for a, engine in enumerate((nc.scalar, nc.sync)):
+            engine.dma_start(out=v_s[a][0:100, :].bitcast(I32), in_=v_s_all[24 + 4 * a : 124 + 4 * a, :].bitcast(I32))
+        deal(nc.vector.tensor_copy, w1_s[0][:], w1_s_raw[:])
+        nc.scalar.dma_start(out=w1_s[1][0:SHIFT_ROWS, :].bitcast(I32), in_=w1_s[0][4 : 4 + SHIFT_ROWS, :].bitcast(I32))
+
+        wr_raw = [new("wr_raw0", [P, PACK, N], F32, "tab_s")]
+        nc.sync.dma_start(out=wr_raw[0][:], in_=wr[0:GROUP, :].rearrange("(p i) n -> p i n", i=PACK))
+        wd_s_raw = w1_s_raw[:, 0:N]
+        load_scale_rows(nc.sync, wd_s_raw, wd_scales)
+
+        for a, lo, hi in ((0, 0, S), (1, 0, FIRST), (1, FIRST, S)):
+            nc.vector.tensor_copy(out=v_w[a][:, lo:hi], in_=tab_w[a][:].bitcast(U32).indirect(offs_sb[:, lo // 16 : hi // 16]))
+
+        for b in range(2):
+            for a in range(PASSES):
+                deal(nc.scalar.copy, w1_w[a][b][:].bitcast(U16), w1_raw[:, a, 2 * GROUP * b : 2 * GROUP * (b + 1)].bitcast(U16))
+
+        wr_raw.append(new("wr_raw1", [P, PACK, N], F32, "tab_w0"))
+        nc.sync.dma_start(out=wr_raw[1][:], in_=wr[GROUP : 2 * GROUP, :].rearrange("(p i) n -> p i n", i=PACK))
+        wd_raw = new("wd_raw", [P, PASSES, N], I32, "w1_raw")
+        nc.sync.dma_start(out=wd_raw[:], in_=wd_words.rearrange("a p c i -> p a (c i)").bitcast(I32))
+
+        def round_wr(b):
+            nc.scalar.activation(
+                out=wr_bf[b][:].rearrange("p (t m i) -> p m t i", t=PACK, i=PACK),
+                in_=wr_raw[b][:].rearrange("p i (m t) -> p m t i", t=PACK),
+                func=ACT.Copy,
+            )
+
+        def quantize(words, scales, src):
+            nc.vector.quantize_mx(out=words.bitcast(FP8X4), scales=scales, in_=src)
+
+        def first_stage(b, j0):
+            bank = h_psum.tile([P, PACK, UNIT], F32, name="h_bank")
+            cols = slice(j0, j0 + UNIT)
+            for i in range(PACK):
+                for a in range(PASSES):
+                    nc.tensor.matmul_mx(
+                        out=bank[:, i, :],
+                        lhsT=w1_w[a][b][:, 2 * P * i : 2 * P * (i + 1)].bitcast(FP4X4),
+                        lhsT_scale=w1_s[a][:, GROUP * b + P * i : GROUP * b + P * (i + 1)],
+                        rhs=v_w[a][:, cols].bitcast(FP8X4),
+                        rhs_scale=v_s[a][:, cols],
+                        start=(a == 0),
+                        stop=(a == PASSES - 1),
+                    )
+            nc.vector.tensor_tensor(
+                out=h_bf[b][:, PACK * j0 : PACK * (j0 + UNIT)].rearrange("p (j i) -> p j i", i=PACK),
+                in0=bank[:].rearrange("p i j -> p j i"),
+                in1=least_sb[:, b, :].unsqueeze(1).broadcast_to([P, UNIT, PACK]),
+                op=ALU.max,
+            )
+
+        def quantize_h(c):
+            lo, hi = CHUNKS[c]
+            for b in range(2):
+                quantize(h_w[b][:, lo:hi], h_s[b][:, lo:hi], h_bf[b][:, PACK * lo : PACK * hi])
+
+        def scores(c, t, words, scales):
+            lo, hi = CHUNKS[c]
+            bank = s_psum.tile([P, 512], F32, name="s_bank")
+            for b in range(2):
+                nc.tensor.matmul_mx(
+                    out=bank[:, 0 : hi - lo],
+                    lhsT=words(b)[:, P * t : P * (t + 1)].bitcast(FP8X4),
+                    lhsT_scale=scales(b)[:, P * t : P * (t + 1)],
+                    rhs=h_w[b][:, lo:hi].bitcast(FP8X4),
+                    rhs_scale=h_s[b][:, lo:hi],
+                    start=(b == 0),
+                    stop=(b == 1),
+                )
+            return bank[:, 0 : hi - lo]
+
+        def response(c, t):
+            lo, hi = CHUNKS[c]
+            acc = scores(c, t, lambda b: wr_w[b], lambda b: wr_s[b])
+            nc.vector.tensor_scalar(
+                out=e_sb[t][:, lo:hi], in0=acc, scalar1=1.0, scalar2=(tops[t][c - 1][:] if c else None),
+                op0=ALU.mult, op1=ALU.max, accum_out=tops[t][c][:],
+            )
+
+        def standby(c, t):
+            lo, hi = CHUNKS[c]
+            acc = scores(c, t, lambda b: wd_w[:, b, :], lambda b: wd_s[4 * b : P, :])
+            nc.scalar.copy(out=d_sb[t][:, lo:hi], in_=acc)
+
+        def units(c):
+            lo, hi = CHUNKS[c]
+            return [(b, j0) for j0 in range(lo, hi, UNIT) for b in range(2)]
+
+        round_wr(0)
+        round_wr(1)
+        deal(nc.scalar.copy, wd_w[:].rearrange("p a c -> p (a c)"), wd_raw[:].rearrange("p a c -> p (a c)").bitcast(U32))
+
+        for u, (b, j0) in enumerate(units(0)):
+            first_stage(b, j0)
+            if u == 3:
+                deal(nc.vector.tensor_copy, wd_s[:], wd_s_raw)
+                quantize(wr_w[0][:], wr_s[0][:], wr_bf[0][:])
+        first_stage(*units(1)[0])
+        quantize_h(0)
+        quantize(wr_w[1][:], wr_s[1][:], wr_bf[1][:])
+        for t in range(PACK):
+            if t:
+                first_stage(*units(1)[t])
+            response(0, t)
+        for t in range(PACK):
+            first_stage(*units(2)[t])
+            if t == 0:
+                quantize_h(1)
+            standby(0, t)
+        for t in range(PACK):
+            response(1, t)
+            if t == 0:
+                quantize_h(2)
+            standby(1, t)
+        last = len(CHUNKS) - 1
+        for t in range(PACK):
+            response(last, t)
+            standby(last, t)
+            nc.scalar.activation(out=neg_top[t][:], in_=tops[t][last][:], func=ACT.Copy, scale=-1.0)
+
+        nc.gpsimd.tensor_tensor(out=gain_base[:], in0=gain_sb[:], in1=base_sb[:], op=ALU.mult)
+        y_rows = out_0.rearrange("(p t) m -> p t m", t=PACK)
+        for t in range(PACK):
+            nc.scalar.activation(out=a_sb[t][:], in_=e_sb[t][:].indirect(pos1_sb[:]), func=ACT.Exp, bias=neg_top[t][:])
+            nc.scalar.activation(out=lift[t][:], in_=a_sb[t][:], func=ACT.Identity, scale=gain_sb[:, t : t + 1], bias=gain_base[:, t : t + 1])
+            nc.vector.tensor_tensor(out=y_sb[:, t, :], in0=d_sb[t][:].indirect(pos2_sb[:]), in1=lift[t][:], op=ALU.mult)
+            nc.sync.dma_start(out=y_rows[:, t, :], in_=y_sb[:, t, :])
+
+        nc.vector.tensor_copy(out=y_bf[:].rearrange("p (m t) -> p m t", t=PACK), in_=y_sb[:].rearrange("p t m -> p m t"))
+        quantize(y_w[:], y_s[:], y_bf[:])
+        nc.sync.dma_start(out=out_1[0].rearrange("p m t -> p (m t)").bitcast(I32), in_=y_w[:].bitcast(I32))
+        for q in range(4):
+            engine = nc.scalar if q % 2 else nc.sync
+            engine.dma_start(out=out_2[0, 4 * q : 4 * q + 4, :].bitcast(I32), in_=y_s[32 * q : 32 * q + 4, :].bitcast(I32))

@@ -21,9 +21,8 @@ PACK = 4
 PASSES = 2
 GROUP = P * PACK
 UNIT = 128
-CHUNKS = ((0, 512), (512, 768), (768, 1024))
-FIRST = 256
-SHIFT_ROWS = 112
+HALF = 512
+HALVES = ((0, HALF), (HALF, S))
 
 
 def tile_list_reserve_activation_scores_kernel(
@@ -42,17 +41,17 @@ def tile_list_reserve_activation_scores_kernel(
         offs_sb = new("offs_sb", [P, S // 16], U16)
         pos1_sb = new("pos1_sb", [P, M // 16], U16)
         pos2_sb = new("pos2_sb", [P, M // 16], U16)
-        tab_w = [new("tab_w%d" % a, [P, T], I32) for a in range(PASSES)]
+        tab_w = [new("tab_w0", [P, T], I32)]
         tab_s = new("tab_s", [P, T], U8)
         v_w = [new("v_w%d" % a, [P, S], U32) for a in range(PASSES)]
         v_s_all = new("v_s_all", [P, S], U8)
-        v_s = [new("v_s%d" % a, [P, S], U8) for a in range(PASSES)]
-        w1_raw = new("w1_raw", [P, PASSES, 2 * H], U8)
+        v_s = new("v_s", [P, PASSES, S], U8)
+        w1_raw = [new("w1_raw0", [P, PASSES, 2 * GROUP], U8)]
         w1_w = [[new("w1_w%d%d" % (a, b), [P, 2 * GROUP], U8) for b in range(2)] for a in range(PASSES)]
-        w1_s_raw = new("w1_s_raw", [P, H], U8)
-        w1_s = [new("w1_s%d" % a, [P, H], U8) for a in range(PASSES)]
+        w_s_raw = new("w_s_raw", [P, H], U8)
+        w_s_all = new("w_s_all", [P, H], U8)
+        w1_s = new("w1_s", [P, PASSES, H], U8)
         wd_w = new("wd_w", [P, PASSES, N], U32)
-        wd_s = new("wd_s", [P, N], U8)
         wr_bf = [new("wr_bf%d" % b, [P, PACK * N], BF16) for b in range(2)]
         wr_w = [new("wr_w%d" % b, [P, N], U32) for b in range(2)]
         wr_s = [new("wr_s%d" % b, [P, N], U8) for b in range(2)]
@@ -65,7 +64,7 @@ def tile_list_reserve_activation_scores_kernel(
         h_s = [new("h_s%d" % b, [P, S], U8) for b in range(2)]
         e_sb = [new("e_sb%d" % t, [P, S], F32) for t in range(PACK)]
         d_sb = [new("d_sb%d" % t, [P, S], F32) for t in range(PACK)]
-        tops = [[new("top%d_%d" % (t, c), [P, 1], F32) for c in range(len(CHUNKS))] for t in range(PACK)]
+        tops = [[new("top%d_%d" % (t, c), [P, 1], F32) for c in range(2)] for t in range(PACK)]
         neg_top = [new("neg_top%d" % t, [P, 1], F32) for t in range(PACK)]
         a_sb = [new("a_sb%d" % t, [P, M], F32) for t in range(PACK)]
         lift = [new("lift%d" % t, [P, M], F32) for t in range(PACK)]
@@ -74,54 +73,59 @@ def tile_list_reserve_activation_scores_kernel(
         y_w = new("y_w", [P, M], U32)
         y_s = new("y_s", [P, M], U8)
 
-        def load_scale_rows(engine, dst, src, row=0):
+        def load_scale_rows(dst, src):
+            nc.sync.dma_start(out=dst.bitcast(I32), in_=src.rearrange("a q c -> q a c").bitcast(I32))
+
+        def spread_scale_rows(engine, planes, rows):
             for q in range(4):
-                engine.dma_start(out=dst[32 * q + row : 32 * q + row + 8, :].bitcast(I32), in_=src[:, 4 * q : 4 * q + 4, :].bitcast(I32))
+                engine.dma_start(out=planes[32 * q : 32 * q + 4, :, :].bitcast(I32), in_=rows[8 * q : 8 * q + 8, :].bitcast(I32))
 
-        def deal(engine_copy, dst, src):
-            engine_copy(out=dst.rearrange("p (g i m) -> p g m i", i=PACK, m=P), in_=src.rearrange("p (g m i) -> p g m i", i=PACK, m=P))
+        def deal(engine_copy, dst, src, walk="p g i m"):
+            engine_copy(out=dst.rearrange("p (g i m) -> " + walk, i=PACK, m=P), in_=src.rearrange("p (g m i) -> " + walk, i=PACK, m=P))
 
-        nc.gpsimd.memset(w1_s_raw[:].bitcast(I32), 0)
-        for q in range(4):
-            engine = nc.vector if q < 2 else nc.gpsimd
-            engine.memset(tab_s[32 * q : 32 * q + 24, :].bitcast(I32), 0)
-        for plane in (v_s[0], v_s[1], w1_s[1]):
-            nc.gpsimd.memset(plane[:].bitcast(I32), 0)
+        nc.vector.memset(w_s_raw[0:64, :].bitcast(I32), 0)
+        nc.vector.memset(w_s_raw[64:96, N:H].bitcast(I32), 0)
+        nc.vector.memset(tab_s[0:96, :].bitcast(I32), 0)
+        nc.gpsimd.memset(w1_s[:].bitcast(I32), 0)
+        nc.gpsimd.memset(v_s[:].bitcast(I32), 0)
 
         nc.sync.dma_start(offs_sb[:], offs)
-        load_scale_rows(nc.sync, tab_s, tab_scales, 24)
-        nc.sync.dma_start(out=tab_w[0][:], in_=tab_words[0].rearrange("p t i -> p (t i)").bitcast(I32))
-        nc.sync.dma_start(out=w1_raw[:].bitcast(I32), in_=w1_words.rearrange("a p c -> p a c").bitcast(I32))
+        load_scale_rows(w_s_raw[96:128, :], w1_scales)
+        load_scale_rows(w_s_raw[64:96, 0:N], wd_scales)
+        load_scale_rows(tab_s[96:128, :], tab_scales)
         nc.sync.dma_start(pos1_sb[:], pos1)
         nc.sync.dma_start(pos2_sb[:], pos2)
-        load_scale_rows(nc.scalar, w1_s_raw, w1_scales)
-        nc.sync.dma_start(out=tab_w[1][:], in_=tab_words[1].rearrange("p t i -> p (t i)").bitcast(I32))
+        nc.sync.dma_start(out=tab_w[0][:], in_=tab_words[0].rearrange("p t i -> p (t i)").bitcast(I32))
+        w1_rows = w1_words.rearrange("a p (b c) -> b p a c", b=2)
+        nc.sync.dma_start(out=w1_raw[0][:].bitcast(I32), in_=w1_rows[0].bitcast(I32))
         nc.gpsimd.dma_start(out=least_sb[:], in_=least.rearrange("(b p i) -> p b i", b=2, i=PACK))
         nc.gpsimd.dma_start(out=base_sb[:], in_=base.rearrange("(p t) -> p t", t=PACK))
         nc.gpsimd.dma_start(out=gain_sb[:], in_=gain.rearrange("(p t) -> p t", t=PACK))
 
+        deal(nc.vector.tensor_copy, w_s_all[:], w_s_raw[:])
+        spread_scale_rows(nc.sync, w1_s, w_s_all[96:128, :])
+        tab_w.append(new("tab_w1", [P, T], I32, "w_s_raw"))
+        nc.sync.dma_start(out=tab_w[1][:], in_=tab_words[1].rearrange("p t i -> p (t i)").bitcast(I32))
         nc.vector.tensor_copy(out=v_s_all[:], in_=tab_s[:].indirect(offs_sb[:]))
-        for a, engine in enumerate((nc.scalar, nc.sync)):
-            engine.dma_start(out=v_s[a][0:100, :].bitcast(I32), in_=v_s_all[24 + 4 * a : 124 + 4 * a, :].bitcast(I32))
-        deal(nc.vector.tensor_copy, w1_s[0][:], w1_s_raw[:])
-        nc.scalar.dma_start(out=w1_s[1][0:SHIFT_ROWS, :].bitcast(I32), in_=w1_s[0][4 : 4 + SHIFT_ROWS, :].bitcast(I32))
+        spread_scale_rows(nc.sync, v_s, v_s_all[96:128, :])
+        w1_raw.append(new("w1_raw1", [P, PASSES, 2 * GROUP], U8, "tab_s"))
+        nc.sync.dma_start(out=w1_raw[1][:].bitcast(I32), in_=w1_rows[1].bitcast(I32))
 
-        wr_raw = [new("wr_raw0", [P, PACK, N], F32, "tab_s")]
-        nc.sync.dma_start(out=wr_raw[0][:], in_=wr[0:GROUP, :].rearrange("(p i) n -> p i n", i=PACK))
-        wd_s_raw = w1_s_raw[:, 0:N]
-        load_scale_rows(nc.sync, wd_s_raw, wd_scales)
-
-        for a, lo, hi in ((0, 0, S), (1, 0, FIRST), (1, FIRST, S)):
+        for a, lo, hi in ((0, 0, HALF), (0, HALF, S), (1, 0, HALF), (1, HALF, S)):
             nc.vector.tensor_copy(out=v_w[a][:, lo:hi], in_=tab_w[a][:].bitcast(U32).indirect(offs_sb[:, lo // 16 : hi // 16]))
 
-        for b in range(2):
-            for a in range(PASSES):
-                deal(nc.scalar.copy, w1_w[a][b][:].bitcast(U16), w1_raw[:, a, 2 * GROUP * b : 2 * GROUP * (b + 1)].bitcast(U16))
+        for a, b in ((0, 0), (1, 0), (0, 1), (1, 1)):
+            deal(nc.scalar.copy, w1_w[a][b][:].bitcast(U16), w1_raw[b][:, a, :].bitcast(U16))
 
-        wr_raw.append(new("wr_raw1", [P, PACK, N], F32, "tab_w0"))
-        nc.sync.dma_start(out=wr_raw[1][:], in_=wr[GROUP : 2 * GROUP, :].rearrange("(p i) n -> p i n", i=PACK))
-        wd_raw = new("wd_raw", [P, PASSES, N], I32, "w1_raw")
+        wr_raw = [new("wr_raw0", [P, PACK, N], F32, "tab_w0")]
+        nc.sync.dma_start(out=wr_raw[0][:], in_=wr[0:GROUP, :].rearrange("(p i) n -> p i n", i=PACK))
+        wd_raw = new("wd_raw", [P, PASSES, N], I32, "w1_raw0")
         nc.sync.dma_start(out=wd_raw[:], in_=wd_words.rearrange("a p c i -> p a (c i)").bitcast(I32))
+        wd_s = new("wd_s", [P, PASSES, N], U8, "v_s_all")
+        nc.gpsimd.memset(wd_s[:].bitcast(I32), 0)
+        spread_scale_rows(nc.sync, wd_s, w_s_all[64:96, 0:N])
+        wr_raw.append(new("wr_raw1", [P, PACK, N], F32, "w_s_raw"))
+        nc.sync.dma_start(out=wr_raw[1][:], in_=wr[GROUP : 2 * GROUP, :].rearrange("(p i) n -> p i n", i=PACK))
 
         def round_wr(b):
             nc.scalar.activation(
@@ -133,20 +137,26 @@ def tile_list_reserve_activation_scores_kernel(
         def quantize(words, scales, src):
             nc.vector.quantize_mx(out=words.bitcast(FP8X4), scales=scales, in_=src)
 
-        def first_stage(b, j0):
-            bank = h_psum.tile([P, PACK, UNIT], F32, name="h_bank")
+        def first_pass(bank, b, j0, a):
             cols = slice(j0, j0 + UNIT)
             for i in range(PACK):
-                for a in range(PASSES):
-                    nc.tensor.matmul_mx(
-                        out=bank[:, i, :],
-                        lhsT=w1_w[a][b][:, 2 * P * i : 2 * P * (i + 1)].bitcast(FP4X4),
-                        lhsT_scale=w1_s[a][:, GROUP * b + P * i : GROUP * b + P * (i + 1)],
-                        rhs=v_w[a][:, cols].bitcast(FP8X4),
-                        rhs_scale=v_s[a][:, cols],
-                        start=(a == 0),
-                        stop=(a == PASSES - 1),
-                    )
+                nc.tensor.matmul_mx(
+                    out=bank[:, i, :],
+                    lhsT=w1_w[a][b][:, 2 * P * i : 2 * P * (i + 1)].bitcast(FP4X4),
+                    lhsT_scale=w1_s[:, a, GROUP * b + P * i : GROUP * b + P * (i + 1)],
+                    rhs=v_w[a][:, cols].bitcast(FP8X4),
+                    rhs_scale=v_s[:, a, cols],
+                    start=(a == 0 and i == 0),
+                    stop=(a == PASSES - 1 and i == PACK - 1),
+                )
+
+        def open_bank(b, j0):
+            bank = h_psum.tile([P, PACK, UNIT], F32, name="h_bank")
+            first_pass(bank, b, j0, 0)
+            return bank
+
+        def close_bank(bank, b, j0):
+            first_pass(bank, b, j0, 1)
             nc.vector.tensor_tensor(
                 out=h_bf[b][:, PACK * j0 : PACK * (j0 + UNIT)].rearrange("p (j i) -> p j i", i=PACK),
                 in0=bank[:].rearrange("p i j -> p j i"),
@@ -154,17 +164,14 @@ def tile_list_reserve_activation_scores_kernel(
                 op=ALU.max,
             )
 
-        def quantize_h(c):
-            lo, hi = CHUNKS[c]
-            for b in range(2):
-                quantize(h_w[b][:, lo:hi], h_s[b][:, lo:hi], h_bf[b][:, PACK * lo : PACK * hi])
+        def quantize_h(b, lo, hi):
+            quantize(h_w[b][:, lo:hi], h_s[b][:, lo:hi], h_bf[b][:, PACK * lo : PACK * hi])
 
-        def scores(c, t, words, scales):
-            lo, hi = CHUNKS[c]
-            bank = s_psum.tile([P, 512], F32, name="s_bank")
+        def scores(c, t, words, scales, bank):
+            lo, hi = HALVES[c]
             for b in range(2):
                 nc.tensor.matmul_mx(
-                    out=bank[:, 0 : hi - lo],
+                    out=bank[:],
                     lhsT=words(b)[:, P * t : P * (t + 1)].bitcast(FP8X4),
                     lhsT_scale=scales(b)[:, P * t : P * (t + 1)],
                     rhs=h_w[b][:, lo:hi].bitcast(FP8X4),
@@ -172,68 +179,81 @@ def tile_list_reserve_activation_scores_kernel(
                     start=(b == 0),
                     stop=(b == 1),
                 )
-            return bank[:, 0 : hi - lo]
+            return bank[:]
 
         def response(c, t):
-            lo, hi = CHUNKS[c]
-            acc = scores(c, t, lambda b: wr_w[b], lambda b: wr_s[b])
+            lo, hi = HALVES[c]
+            acc = scores(c, t, lambda b: wr_w[b], lambda b: wr_s[b], s_psum.tile([P, HALF], F32, name="s_bank"))
             nc.vector.tensor_scalar(
                 out=e_sb[t][:, lo:hi], in0=acc, scalar1=1.0, scalar2=(tops[t][c - 1][:] if c else None),
                 op0=ALU.mult, op1=ALU.max, accum_out=tops[t][c][:],
             )
 
         def standby(c, t):
-            lo, hi = CHUNKS[c]
-            acc = scores(c, t, lambda b: wd_w[:, b, :], lambda b: wd_s[4 * b : P, :])
+            lo, hi = HALVES[c]
+            bank = h_psum.tile([P, HALF], F32, name="h_bank") if c else s_psum.tile([P, HALF], F32, name="s_bank")
+            acc = scores(c, t, lambda b: wd_w[:, b, :], lambda b: wd_s[:, b, :], bank)
             nc.scalar.copy(out=d_sb[t][:, lo:hi], in_=acc)
 
-        def units(c):
-            lo, hi = CHUNKS[c]
-            return [(b, j0) for j0 in range(lo, hi, UNIT) for b in range(2)]
-
         round_wr(0)
+        deal(nc.scalar.copy, wd_w[:].rearrange("p a c -> p (a c)"), wd_raw[:].rearrange("p a c -> p (a c)").bitcast(U32), "p g m i")
         round_wr(1)
-        deal(nc.scalar.copy, wd_w[:].rearrange("p a c -> p (a c)"), wd_raw[:].rearrange("p a c -> p (a c)").bitcast(U32))
 
-        for u, (b, j0) in enumerate(units(0)):
-            first_stage(b, j0)
-            if u == 3:
-                deal(nc.vector.tensor_copy, wd_s[:], wd_s_raw)
-                quantize(wr_w[0][:], wr_s[0][:], wr_bf[0][:])
-        first_stage(*units(1)[0])
-        quantize_h(0)
+        early = [(0, j0) for j0 in range(0, 2 * UNIT, UNIT)]
+        banks = [open_bank(b, j0) for b, j0 in early]
+        for bank, (b, j0) in zip(banks, early):
+            close_bank(bank, b, j0)
+
+        def first_stage(b, lo, hi):
+            for j0 in range(lo, hi, UNIT):
+                close_bank(open_bank(b, j0), b, j0)
+
+        first_stage(0, 2 * UNIT, HALF)
+        first_stage(1, 0, UNIT)
+        quantize_h(0, 0, HALF)
+        first_stage(1, UNIT, HALF)
+        quantize_h(1, 0, HALF)
+        first_stage(0, HALF, S)
+        quantize(wr_w[0][:], wr_s[0][:], wr_bf[0][:])
+        quantize_h(0, HALF, S)
+        first_stage(1, HALF, 896)
         quantize(wr_w[1][:], wr_s[1][:], wr_bf[1][:])
+        quantize_h(1, HALF, 768)
+        first_stage(1, 896, S)
+        for t in range(PACK):
+            standby(0, t)
+        response(0, 0)
+        quantize_h(1, 768, S)
         for t in range(PACK):
             if t:
-                first_stage(*units(1)[t])
-            response(0, t)
-        for t in range(PACK):
-            first_stage(*units(2)[t])
-            if t == 0:
-                quantize_h(1)
-            standby(0, t)
-        for t in range(PACK):
+                response(0, t)
             response(1, t)
-            if t == 0:
-                quantize_h(2)
-            standby(1, t)
-        last = len(CHUNKS) - 1
-        for t in range(PACK):
-            response(last, t)
-            standby(last, t)
-            nc.scalar.activation(out=neg_top[t][:], in_=tops[t][last][:], func=ACT.Copy, scale=-1.0)
+            nc.scalar.activation(out=neg_top[t][:], in_=tops[t][1][:], func=ACT.Copy, scale=-1.0)
 
         nc.gpsimd.tensor_tensor(out=gain_base[:], in0=gain_sb[:], in1=base_sb[:], op=ALU.mult)
         y_rows = out_0.rearrange("(p t) m -> p t m", t=PACK)
         for t in range(PACK):
             nc.scalar.activation(out=a_sb[t][:], in_=e_sb[t][:].indirect(pos1_sb[:]), func=ACT.Exp, bias=neg_top[t][:])
-            nc.scalar.activation(out=lift[t][:], in_=a_sb[t][:], func=ACT.Identity, scale=gain_sb[:, t : t + 1], bias=gain_base[:, t : t + 1])
-            nc.vector.tensor_tensor(out=y_sb[:, t, :], in0=d_sb[t][:].indirect(pos2_sb[:]), in1=lift[t][:], op=ALU.mult)
+            standby(1, t)
+            if t < 2:
+                nc.scalar.activation(out=lift[t][:], in_=a_sb[t][:], func=ACT.Identity, scale=gain_sb[:, t : t + 1], bias=gain_base[:, t : t + 1])
+            else:
+                nc.vector.tensor_scalar(
+                    out=lift[t][:], in0=a_sb[t][:], scalar1=base_sb[:, t : t + 1], scalar2=gain_sb[:, t : t + 1],
+                    op0=ALU.add, op1=ALU.mult,
+                )
+            for lo, hi in ((0, M),) if t < PACK - 1 else ((0, M // 2), (M // 2, M)):
+                nc.vector.tensor_tensor(
+                    out=y_sb[:, t, lo:hi], in0=d_sb[t][:].indirect(pos2_sb[:, lo // 16 : hi // 16]), in1=lift[t][:, lo:hi], op=ALU.mult
+                )
             nc.sync.dma_start(out=y_rows[:, t, :], in_=y_sb[:, t, :])
 
-        nc.vector.tensor_copy(out=y_bf[:].rearrange("p (m t) -> p m t", t=PACK), in_=y_sb[:].rearrange("p t m -> p m t"))
-        quantize(y_w[:], y_s[:], y_bf[:])
-        nc.sync.dma_start(out=out_1[0].rearrange("p m t -> p (m t)").bitcast(I32), in_=y_w[:].bitcast(I32))
+        y_words = out_1[0].rearrange("p m t -> p (m t)").bitcast(I32)
+        for copy, lo, hi in ((nc.scalar.copy, 0, M // 2), (nc.vector.tensor_copy, M // 2, M)):
+            copy(out=y_bf[:, PACK * lo : PACK * hi].rearrange("p (m t) -> p m t", t=PACK), in_=y_sb[:, :, lo:hi].rearrange("p t m -> p m t"))
+        for lo, hi in ((M // 2, M), (0, M // 2)):
+            quantize(y_w[:, lo:hi], y_s[:, lo:hi], y_bf[:, PACK * lo : PACK * hi])
+            nc.sync.dma_start(out=y_words[:, lo:hi], in_=y_w[:, lo:hi].bitcast(I32))
         for q in range(4):
             engine = nc.scalar if q % 2 else nc.sync
             engine.dma_start(out=out_2[0, 4 * q : 4 * q + 4, :].bitcast(I32), in_=y_s[32 * q : 32 * q + 4, :].bitcast(I32))

@@ -18,11 +18,18 @@ ACT = mybir.ActivationFunctionType
 
 P = 128
 PACK = 4
-PASSES = 2
 GROUP = P * PACK
+K_GROUPS = K // GROUP
+R_GROUPS = H // GROUP
+QUADRANTS = 4
+LIST_ROWS = 16
 UNIT = 128
 HALF = 512
 HALVES = ((0, HALF), (HALF, S))
+Y_HALVES = ((0, M // 2), (M // 2, M))
+BANKS = 4
+BANKS_AHEAD = 2
+LIFTS_ON_SCALAR = 2
 
 
 def tile_list_reserve_activation_scores_kernel(
@@ -32,98 +39,111 @@ def tile_list_reserve_activation_scores_kernel(
     nc = tc.nc
     with ExitStack() as ctx:
         keep = ctx.enter_context(tc.tile_pool(name="keep", bufs=1))
-        h_psum = ctx.enter_context(tc.psum_pool(name="h_psum", bufs=4))
-        s_psum = ctx.enter_context(tc.psum_pool(name="s_psum", bufs=4))
+        h_psum = ctx.enter_context(tc.psum_pool(name="h_psum", bufs=BANKS))
+        s_psum = ctx.enter_context(tc.psum_pool(name="s_psum", bufs=BANKS))
 
         def new(name, shape, dtype, tag=None):
             return keep.tile(shape, dtype, name=name, tag=tag or name, align_bytes=64)
 
-        offs_sb = new("offs_sb", [P, S // 16], U16)
-        pos1_sb = new("pos1_sb", [P, M // 16], U16)
-        pos2_sb = new("pos2_sb", [P, M // 16], U16)
+        offs_sb = new("offs_sb", [P, S // LIST_ROWS], U16)
+        pos1_sb = new("pos1_sb", [P, M // LIST_ROWS], U16)
+        pos2_sb = new("pos2_sb", [P, M // LIST_ROWS], U16)
         tab_w = [new("tab_w0", [P, T], I32)]
         tab_s = new("tab_s", [P, T], U8)
-        v_w = [new("v_w%d" % a, [P, S], U32) for a in range(PASSES)]
-        v_s_all = new("v_s_all", [P, S], U8)
-        v_s = new("v_s", [P, PASSES, S], U8)
-        w1_raw = [new("w1_raw0", [P, PASSES, 2 * GROUP], U8)]
-        w1_w = [[new("w1_w%d%d" % (a, b), [P, 2 * GROUP], U8) for b in range(2)] for a in range(PASSES)]
+        v_w = [new("v_w%d" % a, [P, S], U32) for a in range(K_GROUPS)]
+        v_s_rows = new("v_s_all", [P, S], U8)
+        v_s = new("v_s", [P, K_GROUPS, S], U8)
+        w1_raw = [new("w1_raw0", [P, K_GROUPS, 2 * GROUP], U8)]
+        w1_w = [[new("w1_w%d%d" % (a, b), [P, 2 * GROUP], U8) for b in range(R_GROUPS)] for a in range(K_GROUPS)]
         w_s_raw = new("w_s_raw", [P, H], U8)
-        w_s_all = new("w_s_all", [P, H], U8)
-        w1_s = new("w1_s", [P, PASSES, H], U8)
-        wd_w = new("wd_w", [P, PASSES, N], U32)
-        wr_bf = [new("wr_bf%d" % b, [P, PACK * N], BF16) for b in range(2)]
-        wr_w = [new("wr_w%d" % b, [P, N], U32) for b in range(2)]
-        wr_s = [new("wr_s%d" % b, [P, N], U8) for b in range(2)]
-        least_sb = new("least_sb", [P, 2, PACK], F32)
+        w_s_rows = new("w_s_all", [P, H], U8)
+        w1_s = new("w1_s", [P, K_GROUPS, H], U8)
+        wd_w = new("wd_w", [P, R_GROUPS, N], U32)
+        wr_bf = [new("wr_bf%d" % b, [P, PACK * N], BF16) for b in range(R_GROUPS)]
+        wr_w = [new("wr_w%d" % b, [P, N], U32) for b in range(R_GROUPS)]
+        wr_s = [new("wr_s%d" % b, [P, N], U8) for b in range(R_GROUPS)]
+        least_sb = new("least_sb", [P, R_GROUPS, PACK], F32)
         base_sb = new("base_sb", [P, PACK], F32)
         gain_sb = new("gain_sb", [P, PACK], F32)
         gain_base = new("gain_base", [P, PACK], F32)
-        h_bf = [new("h_bf%d" % b, [P, PACK * S], BF16) for b in range(2)]
-        h_w = [new("h_w%d" % b, [P, S], U32) for b in range(2)]
-        h_s = [new("h_s%d" % b, [P, S], U8) for b in range(2)]
+        h_bf = [new("h_bf%d" % b, [P, PACK * S], BF16) for b in range(R_GROUPS)]
+        h_w = [new("h_w%d" % b, [P, S], U32) for b in range(R_GROUPS)]
+        h_s = [new("h_s%d" % b, [P, S], U8) for b in range(R_GROUPS)]
         e_sb = [new("e_sb%d" % t, [P, S], F32) for t in range(PACK)]
         d_sb = [new("d_sb%d" % t, [P, S], F32) for t in range(PACK)]
-        tops = [[new("top%d_%d" % (t, c), [P, 1], F32) for c in range(2)] for t in range(PACK)]
+        tops = [[new("top%d_%d" % (t, c), [P, 1], F32) for c in range(len(HALVES))] for t in range(PACK)]
         neg_top = [new("neg_top%d" % t, [P, 1], F32) for t in range(PACK)]
         a_sb = [new("a_sb%d" % t, [P, M], F32) for t in range(PACK)]
         lift = [new("lift%d" % t, [P, M], F32) for t in range(PACK)]
-        y_sb = new("y_sb", [P, PACK, M], F32)
+        y_sb = [new("y_sb%d" % g, [P, PACK, M // 2], F32) for g in range(len(Y_HALVES))]
         y_bf = new("y_bf", [P, PACK * M], BF16)
         y_w = new("y_w", [P, M], U32)
         y_s = new("y_s", [P, M], U8)
 
-        def load_scale_rows(dst, src):
-            nc.sync.dma_start(out=dst.bitcast(I32), in_=src.rearrange("a q c -> q a c").bitcast(I32))
+        last_quadrant, third_quadrant = slice(96, 128), slice(64, 96)
 
-        def spread_scale_rows(engine, planes, rows):
-            for q in range(4):
-                engine.dma_start(out=planes[32 * q : 32 * q + 4, :, :].bitcast(I32), in_=rows[8 * q : 8 * q + 8, :].bitcast(I32))
+        def entries(offsets, lo, hi):
+            return offsets[:, lo // LIST_ROWS : hi // LIST_ROWS]
+
+        def load_scale_rows(rows, src):
+            nc.sync.dma_start(out=rows.bitcast(I32), in_=src.rearrange("g q c -> q g c").bitcast(I32))
+
+        def spread_scale_rows(planes, rows):
+            for quad in range(QUADRANTS):
+                nc.sync.dma_start(
+                    out=planes[32 * quad : 32 * quad + 4, :, :].bitcast(I32),
+                    in_=rows[8 * quad : 8 * quad + 8, :].bitcast(I32),
+                )
 
         def deal(engine_copy, dst, src, walk="p g i m"):
-            engine_copy(out=dst.rearrange("p (g i m) -> " + walk, i=PACK, m=P), in_=src.rearrange("p (g m i) -> " + walk, i=PACK, m=P))
+            engine_copy(
+                out=dst.rearrange("p (g i m) -> " + walk, i=PACK, m=P),
+                in_=src.rearrange("p (g m i) -> " + walk, i=PACK, m=P),
+            )
 
         nc.vector.memset(w_s_raw[0:64, :].bitcast(I32), 0)
-        nc.vector.memset(w_s_raw[64:96, N:H].bitcast(I32), 0)
+        nc.vector.memset(w_s_raw[third_quadrant, N:H].bitcast(I32), 0)
         nc.vector.memset(tab_s[0:96, :].bitcast(I32), 0)
         nc.gpsimd.memset(w1_s[:].bitcast(I32), 0)
         nc.gpsimd.memset(v_s[:].bitcast(I32), 0)
 
         nc.sync.dma_start(offs_sb[:], offs)
-        load_scale_rows(w_s_raw[96:128, :], w1_scales)
-        load_scale_rows(w_s_raw[64:96, 0:N], wd_scales)
-        load_scale_rows(tab_s[96:128, :], tab_scales)
+        load_scale_rows(w_s_raw[last_quadrant, :], w1_scales)
+        load_scale_rows(w_s_raw[third_quadrant, 0:N], wd_scales)
+        load_scale_rows(tab_s[last_quadrant, :], tab_scales)
         nc.sync.dma_start(pos1_sb[:], pos1)
         nc.sync.dma_start(pos2_sb[:], pos2)
         nc.sync.dma_start(out=tab_w[0][:], in_=tab_words[0].rearrange("p t i -> p (t i)").bitcast(I32))
-        w1_rows = w1_words.rearrange("a p (b c) -> b p a c", b=2)
-        nc.sync.dma_start(out=w1_raw[0][:].bitcast(I32), in_=w1_rows[0].bitcast(I32))
-        nc.gpsimd.dma_start(out=least_sb[:], in_=least.rearrange("(b p i) -> p b i", b=2, i=PACK))
+        w1_by_group = w1_words.rearrange("a p (b c) -> b p a c", b=R_GROUPS)
+        nc.sync.dma_start(out=w1_raw[0][:].bitcast(I32), in_=w1_by_group[0].bitcast(I32))
+        nc.gpsimd.dma_start(out=least_sb[:], in_=least.rearrange("(b p i) -> p b i", b=R_GROUPS, i=PACK))
         nc.gpsimd.dma_start(out=base_sb[:], in_=base.rearrange("(p t) -> p t", t=PACK))
         nc.gpsimd.dma_start(out=gain_sb[:], in_=gain.rearrange("(p t) -> p t", t=PACK))
 
-        deal(nc.vector.tensor_copy, w_s_all[:], w_s_raw[:])
-        spread_scale_rows(nc.sync, w1_s, w_s_all[96:128, :])
+        deal(nc.vector.tensor_copy, w_s_rows[:], w_s_raw[:])
+        spread_scale_rows(w1_s, w_s_rows[last_quadrant, :])
         tab_w.append(new("tab_w1", [P, T], I32, "w_s_raw"))
         nc.sync.dma_start(out=tab_w[1][:], in_=tab_words[1].rearrange("p t i -> p (t i)").bitcast(I32))
-        nc.vector.tensor_copy(out=v_s_all[:], in_=tab_s[:].indirect(offs_sb[:]))
-        spread_scale_rows(nc.sync, v_s, v_s_all[96:128, :])
-        w1_raw.append(new("w1_raw1", [P, PASSES, 2 * GROUP], U8, "tab_s"))
-        nc.sync.dma_start(out=w1_raw[1][:].bitcast(I32), in_=w1_rows[1].bitcast(I32))
+        nc.vector.tensor_copy(out=v_s_rows[:], in_=tab_s[:].indirect(offs_sb[:]))
+        spread_scale_rows(v_s, v_s_rows[last_quadrant, :])
+        w1_raw.append(new("w1_raw1", [P, K_GROUPS, 2 * GROUP], U8, "tab_s"))
+        nc.sync.dma_start(out=w1_raw[1][:].bitcast(I32), in_=w1_by_group[1].bitcast(I32))
 
-        for a, lo, hi in ((0, 0, HALF), (0, HALF, S), (1, 0, HALF), (1, HALF, S)):
-            nc.vector.tensor_copy(out=v_w[a][:, lo:hi], in_=tab_w[a][:].bitcast(U32).indirect(offs_sb[:, lo // 16 : hi // 16]))
+        for a in range(K_GROUPS):
+            for lo, hi in HALVES:
+                nc.vector.tensor_copy(out=v_w[a][:, lo:hi], in_=tab_w[a][:].bitcast(U32).indirect(entries(offs_sb, lo, hi)))
 
-        for a, b in ((0, 0), (1, 0), (0, 1), (1, 1)):
-            deal(nc.scalar.copy, w1_w[a][b][:].bitcast(U16), w1_raw[b][:, a, :].bitcast(U16))
+        for b in range(R_GROUPS):
+            for a in range(K_GROUPS):
+                deal(nc.scalar.copy, w1_w[a][b][:].bitcast(U16), w1_raw[b][:, a, :].bitcast(U16))
 
         wr_raw = [new("wr_raw0", [P, PACK, N], F32, "tab_w0")]
         nc.sync.dma_start(out=wr_raw[0][:], in_=wr[0:GROUP, :].rearrange("(p i) n -> p i n", i=PACK))
-        wd_raw = new("wd_raw", [P, PASSES, N], I32, "w1_raw0")
-        nc.sync.dma_start(out=wd_raw[:], in_=wd_words.rearrange("a p c i -> p a (c i)").bitcast(I32))
-        wd_s = new("wd_s", [P, PASSES, N], U8, "v_s_all")
+        wd_raw = new("wd_raw", [P, R_GROUPS, N], I32, "w1_raw0")
+        nc.sync.dma_start(out=wd_raw[:], in_=wd_words.rearrange("b p c i -> p b (c i)").bitcast(I32))
+        wd_s = new("wd_s", [P, R_GROUPS, N], U8, "v_s_all")
         nc.gpsimd.memset(wd_s[:].bitcast(I32), 0)
-        spread_scale_rows(nc.sync, wd_s, w_s_all[64:96, 0:N])
+        spread_scale_rows(wd_s, w_s_rows[third_quadrant, 0:N])
         wr_raw.append(new("wr_raw1", [P, PACK, N], F32, "w_s_raw"))
         nc.sync.dma_start(out=wr_raw[1][:], in_=wr[GROUP : 2 * GROUP, :].rearrange("(p i) n -> p i n", i=PACK))
 
@@ -137,7 +157,7 @@ def tile_list_reserve_activation_scores_kernel(
         def quantize(words, scales, src):
             nc.vector.quantize_mx(out=words.bitcast(FP8X4), scales=scales, in_=src)
 
-        def first_pass(bank, b, j0, a):
+        def first_stage_pass(bank, b, j0, a):
             cols = slice(j0, j0 + UNIT)
             for i in range(PACK):
                 nc.tensor.matmul_mx(
@@ -147,16 +167,16 @@ def tile_list_reserve_activation_scores_kernel(
                     rhs=v_w[a][:, cols].bitcast(FP8X4),
                     rhs_scale=v_s[:, a, cols],
                     start=(a == 0 and i == 0),
-                    stop=(a == PASSES - 1 and i == PACK - 1),
+                    stop=(a == K_GROUPS - 1 and i == PACK - 1),
                 )
 
         def open_bank(b, j0):
             bank = h_psum.tile([P, PACK, UNIT], F32, name="h_bank")
-            first_pass(bank, b, j0, 0)
+            first_stage_pass(bank, b, j0, 0)
             return bank
 
         def close_bank(bank, b, j0):
-            first_pass(bank, b, j0, 1)
+            first_stage_pass(bank, b, j0, 1)
             nc.vector.tensor_tensor(
                 out=h_bf[b][:, PACK * j0 : PACK * (j0 + UNIT)].rearrange("p (j i) -> p j i", i=PACK),
                 in0=bank[:].rearrange("p i j -> p j i"),
@@ -164,96 +184,106 @@ def tile_list_reserve_activation_scores_kernel(
                 op=ALU.max,
             )
 
+        def first_stage(b, lo, hi):
+            for j0 in range(lo, hi, UNIT):
+                close_bank(open_bank(b, j0), b, j0)
+
         def quantize_h(b, lo, hi):
             quantize(h_w[b][:, lo:hi], h_s[b][:, lo:hi], h_bf[b][:, PACK * lo : PACK * hi])
 
-        def scores(c, t, words, scales, bank):
+        def quantize_wr(b):
+            quantize(wr_w[b][:], wr_s[b][:], wr_bf[b][:])
+
+        def scores(bank, c, t, words, scales):
             lo, hi = HALVES[c]
-            for b in range(2):
+            for b in range(R_GROUPS):
                 nc.tensor.matmul_mx(
                     out=bank[:],
-                    lhsT=words(b)[:, P * t : P * (t + 1)].bitcast(FP8X4),
-                    lhsT_scale=scales(b)[:, P * t : P * (t + 1)],
+                    lhsT=words[b][:, P * t : P * (t + 1)].bitcast(FP8X4),
+                    lhsT_scale=scales[b][:, P * t : P * (t + 1)],
                     rhs=h_w[b][:, lo:hi].bitcast(FP8X4),
                     rhs_scale=h_s[b][:, lo:hi],
                     start=(b == 0),
-                    stop=(b == 1),
+                    stop=(b == R_GROUPS - 1),
                 )
-            return bank[:]
 
         def response(c, t):
             lo, hi = HALVES[c]
-            acc = scores(c, t, lambda b: wr_w[b], lambda b: wr_s[b], s_psum.tile([P, HALF], F32, name="s_bank"))
+            bank = s_psum.tile([P, HALF], F32, name="s_bank")
+            scores(bank, c, t, wr_w, wr_s)
             nc.vector.tensor_scalar(
-                out=e_sb[t][:, lo:hi], in0=acc, scalar1=1.0, scalar2=(tops[t][c - 1][:] if c else None),
+                out=e_sb[t][:, lo:hi], in0=bank[:], scalar1=1.0, scalar2=(tops[t][c - 1][:] if c else None),
                 op0=ALU.mult, op1=ALU.max, accum_out=tops[t][c][:],
             )
 
         def standby(c, t):
             lo, hi = HALVES[c]
             bank = h_psum.tile([P, HALF], F32, name="h_bank") if c else s_psum.tile([P, HALF], F32, name="s_bank")
-            acc = scores(c, t, lambda b: wd_w[:, b, :], lambda b: wd_s[:, b, :], bank)
-            nc.scalar.copy(out=d_sb[t][:, lo:hi], in_=acc)
+            scores(bank, c, t, [wd_w[:, b, :] for b in range(R_GROUPS)], [wd_s[:, b, :] for b in range(R_GROUPS)])
+            nc.scalar.copy(out=d_sb[t][:, lo:hi], in_=bank[:])
 
         round_wr(0)
-        deal(nc.scalar.copy, wd_w[:].rearrange("p a c -> p (a c)"), wd_raw[:].rearrange("p a c -> p (a c)").bitcast(U32), "p g m i")
+        deal(nc.scalar.copy, wd_w[:].rearrange("p b c -> p (b c)"), wd_raw[:].rearrange("p b c -> p (b c)").bitcast(U32), "p g m i")
         round_wr(1)
 
-        early = [(0, j0) for j0 in range(0, 2 * UNIT, UNIT)]
-        banks = [open_bank(b, j0) for b, j0 in early]
-        for bank, (b, j0) in zip(banks, early):
-            close_bank(bank, b, j0)
-
-        def first_stage(b, lo, hi):
-            for j0 in range(lo, hi, UNIT):
-                close_bank(open_bank(b, j0), b, j0)
-
-        first_stage(0, 2 * UNIT, HALF)
+        ahead = [(open_bank(0, j0), 0, j0) for j0 in range(0, BANKS_AHEAD * UNIT, UNIT)]
+        for bank_and_place in ahead:
+            close_bank(*bank_and_place)
+        first_stage(0, BANKS_AHEAD * UNIT, HALF)
         first_stage(1, 0, UNIT)
         quantize_h(0, 0, HALF)
         first_stage(1, UNIT, HALF)
+        first_stage(0, HALF, HALF + UNIT)
         quantize_h(1, 0, HALF)
-        first_stage(0, HALF, S)
-        quantize(wr_w[0][:], wr_s[0][:], wr_bf[0][:])
+        first_stage(0, HALF + UNIT, S)
+        first_stage(1, HALF, HALF + UNIT)
         quantize_h(0, HALF, S)
-        first_stage(1, HALF, 896)
-        quantize(wr_w[1][:], wr_s[1][:], wr_bf[1][:])
-        quantize_h(1, HALF, 768)
-        first_stage(1, 896, S)
+        quantize_wr(0)
+        first_stage(1, HALF + UNIT, S - UNIT)
+        quantize_h(1, HALF, S - 2 * UNIT)
+        quantize_wr(1)
+        first_stage(1, S - UNIT, S)
         for t in range(PACK):
             standby(0, t)
         response(0, 0)
-        quantize_h(1, 768, S)
+        quantize_h(1, S - 2 * UNIT, S)
+
         for t in range(PACK):
-            if t:
-                response(0, t)
+            if t + 1 < PACK:
+                response(0, t + 1)
             response(1, t)
             nc.scalar.activation(out=neg_top[t][:], in_=tops[t][1][:], func=ACT.Copy, scale=-1.0)
+            if t + 1 == PACK // 2:
+                standby(1, 0)
 
         nc.gpsimd.tensor_tensor(out=gain_base[:], in0=gain_sb[:], in1=base_sb[:], op=ALU.mult)
         y_rows = out_0.rearrange("(p t) m -> p t m", t=PACK)
         for t in range(PACK):
             nc.scalar.activation(out=a_sb[t][:], in_=e_sb[t][:].indirect(pos1_sb[:]), func=ACT.Exp, bias=neg_top[t][:])
-            standby(1, t)
-            if t < 2:
-                nc.scalar.activation(out=lift[t][:], in_=a_sb[t][:], func=ACT.Identity, scale=gain_sb[:, t : t + 1], bias=gain_base[:, t : t + 1])
+            if t > 0:
+                standby(1, t)
+            if t < LIFTS_ON_SCALAR:
+                nc.scalar.activation(
+                    out=lift[t][:], in_=a_sb[t][:], func=ACT.Identity,
+                    scale=gain_sb[:, t : t + 1], bias=gain_base[:, t : t + 1],
+                )
             else:
                 nc.vector.tensor_scalar(
                     out=lift[t][:], in0=a_sb[t][:], scalar1=base_sb[:, t : t + 1], scalar2=gain_sb[:, t : t + 1],
                     op0=ALU.add, op1=ALU.mult,
                 )
-            for lo, hi in ((0, M),) if t < PACK - 1 else ((0, M // 2), (M // 2, M)):
+            for y_half, (lo, hi) in zip(y_sb, Y_HALVES):
                 nc.vector.tensor_tensor(
-                    out=y_sb[:, t, lo:hi], in0=d_sb[t][:].indirect(pos2_sb[:, lo // 16 : hi // 16]), in1=lift[t][:, lo:hi], op=ALU.mult
+                    out=y_half[:, t, :], in0=d_sb[t][:].indirect(entries(pos2_sb, lo, hi)), in1=lift[t][:, lo:hi], op=ALU.mult
                 )
-            nc.sync.dma_start(out=y_rows[:, t, :], in_=y_sb[:, t, :])
+                nc.sync.dma_start(out=y_rows[:, t, lo:hi], in_=y_half[:, t, :])
 
         y_words = out_1[0].rearrange("p m t -> p (m t)").bitcast(I32)
-        for copy, lo, hi in ((nc.scalar.copy, 0, M // 2), (nc.vector.tensor_copy, M // 2, M)):
-            copy(out=y_bf[:, PACK * lo : PACK * hi].rearrange("p (m t) -> p m t", t=PACK), in_=y_sb[:, :, lo:hi].rearrange("p t m -> p m t"))
-        for lo, hi in ((M // 2, M), (0, M // 2)):
+        for copy, y_half, (lo, hi) in zip((nc.scalar.copy, nc.vector.tensor_copy), y_sb, Y_HALVES):
+            copy(out=y_bf[:, PACK * lo : PACK * hi].rearrange("p (m t) -> p m t", t=PACK), in_=y_half[:].rearrange("p t m -> p m t"))
+        for lo, hi in Y_HALVES:
             quantize(y_w[:, lo:hi], y_s[:, lo:hi], y_bf[:, PACK * lo : PACK * hi])
             nc.sync.dma_start(out=y_words[:, lo:hi], in_=y_w[:, lo:hi].bitcast(I32))
-        for q in range(4):
-            engine = nc.scalar if q % 2 else nc.sync
-            engine.dma_start(out=out_2[0, 4 * q : 4 * q + 4, :].bitcast(I32), in_=y_s[32 * q : 32 * q + 4, :].bitcast(I32))
+        for quad in range(QUADRANTS):
+            engine = nc.scalar if quad % 2 else nc.sync
+            engine.dma_start(out=out_2[0, 4 * quad : 4 * quad + 4, :].bitcast(I32), in_=y_s[32 * quad : 32 * quad + 4, :].bitcast(I32))

from contextlib import ExitStack

import concourse.mybir as mybir

K, H, N, T, S, M = 1024, 1024, 512, 2048, 1024, 512
FLOPS = 2 * K * H * S + 4 * H * N * S

F32 = mybir.dt.float32
BF16 = mybir.dt.bfloat16
I32 = mybir.dt.int32
U32 = mybir.dt.uint32
U16 = mybir.dt.uint16
U8 = mybir.dt.uint8
FP8X4 = mybir.dt.float8_e4m3fn_x4
FP4X4 = mybir.dt.float4_e2m1fn_x4
ALU = mybir.AluOpType
ACT = mybir.ActivationFunctionType

P = 128
PACK = 4
GROUP = P * PACK
K_GROUPS = K // GROUP
R_GROUPS = H // GROUP
QUADRANTS = 4
LIST_ROWS = 16
UNIT = 128
HALF = 512
HALVES = ((0, HALF), (HALF, S))
Y_HALVES = ((0, M // 2), (M // 2, M))
BANKS = 4
BANKS_AHEAD = 2
LIFTS_ON_SCALAR = 2


def tile_list_reserve_activation_scores_kernel(
    tc, tab_words, tab_scales, offs, pos1, pos2, w1_words, w1_scales, least, wr, wd_words, wd_scales, base, gain,
    out_0, out_1, out_2,
):
    nc = tc.nc
    with ExitStack() as ctx:
        keep = ctx.enter_context(tc.tile_pool(name="keep", bufs=1))
        h_psum = ctx.enter_context(tc.psum_pool(name="h_psum", bufs=BANKS))
        s_psum = ctx.enter_context(tc.psum_pool(name="s_psum", bufs=BANKS))

        def new(name, shape, dtype, tag=None):
            return keep.tile(shape, dtype, name=name, tag=tag or name, align_bytes=64)

        offs_sb = new("offs_sb", [P, S // LIST_ROWS], U16)
        pos1_sb = new("pos1_sb", [P, M // LIST_ROWS], U16)
        pos2_sb = new("pos2_sb", [P, M // LIST_ROWS], U16)
        tab_w = [new("tab_w0", [P, T], I32)]
        tab_s = new("tab_s", [P, T], U8)
        v_w = [new("v_w%d" % a, [P, S], U32) for a in range(K_GROUPS)]
        v_s_rows = new("v_s_all", [P, S], U8)
        v_s = new("v_s", [P, K_GROUPS, S], U8)
        w1_raw = [new("w1_raw0", [P, K_GROUPS, 2 * GROUP], U8)]
        w1_w = [[new("w1_w%d%d" % (a, b), [P, 2 * GROUP], U8) for b in range(R_GROUPS)] for a in range(K_GROUPS)]
        w_s_raw = new("w_s_raw", [P, H], U8)
        w_s_rows = new("w_s_all", [P, H], U8)
        w1_s = new("w1_s", [P, K_GROUPS, H], U8)
        wd_w = new("wd_w", [P, R_GROUPS, N], U32)
        wr_bf = [new("wr_bf%d" % b, [P, PACK * N], BF16) for b in range(R_GROUPS)]
        wr_w = [new("wr_w%d" % b, [P, N], U32) for b in range(R_GROUPS)]
        wr_s = [new("wr_s%d" % b, [P, N], U8) for b in range(R_GROUPS)]
        least_sb = new("least_sb", [P, R_GROUPS, PACK], F32)
        base_sb = new("base_sb", [P, PACK], F32)
        gain_sb = new("gain_sb", [P, PACK], F32)
        gain_base = new("gain_base", [P, PACK], F32)
        h_bf = [new("h_bf%d" % b, [P, PACK * S], BF16) for b in range(R_GROUPS)]
        h_w = [new("h_w%d" % b, [P, S], U32) for b in range(R_GROUPS)]
        h_s = [new("h_s%d" % b, [P, S], U8) for b in range(R_GROUPS)]
        e_sb = [new("e_sb%d" % t, [P, S], F32) for t in range(PACK)]
        d_sb = [new("d_sb%d" % t, [P, S], F32) for t in range(PACK)]
        tops = [[new("top%d_%d" % (t, c), [P, 1], F32) for c in range(len(HALVES))] for t in range(PACK)]
        neg_top = [new("neg_top%d" % t, [P, 1], F32) for t in range(PACK)]
        a_sb = [new("a_sb%d" % t, [P, M], F32) for t in range(PACK)]
        lift = [new("lift%d" % t, [P, M], F32) for t in range(PACK)]
        y_sb = [new("y_sb%d" % g, [P, PACK, M // 2], F32) for g in range(len(Y_HALVES))]
        y_bf = new("y_bf", [P, PACK * M], BF16)
        y_w = new("y_w", [P, M], U32)
        y_s = new("y_s", [P, M], U8)

        last_quadrant, third_quadrant = slice(96, 128), slice(64, 96)

        def entries(offsets, lo, hi):
            return offsets[:, lo // LIST_ROWS : hi // LIST_ROWS]

        def load_scale_rows(rows, src):
            nc.sync.dma_start(out=rows.bitcast(I32), in_=src.rearrange("g q c -> q g c").bitcast(I32))

        def spread_scale_rows(planes, rows):
            for quad in range(QUADRANTS):
                nc.sync.dma_start(
                    out=planes[32 * quad : 32 * quad + 4, :, :].bitcast(I32),
                    in_=rows[8 * quad : 8 * quad + 8, :].bitcast(I32),
                )

        def deal(engine_copy, dst, src, walk="p g i m"):
            engine_copy(
                out=dst.rearrange("p (g i m) -> " + walk, i=PACK, m=P),
                in_=src.rearrange("p (g m i) -> " + walk, i=PACK, m=P),
            )

        nc.vector.memset(w_s_raw[0:64, :].bitcast(I32), 0)
        nc.vector.memset(w_s_raw[third_quadrant, N:H].bitcast(I32), 0)
        nc.vector.memset(tab_s[0:96, :].bitcast(I32), 0)
        nc.gpsimd.memset(w1_s[:].bitcast(I32), 0)
        nc.gpsimd.memset(v_s[:].bitcast(I32), 0)

        nc.sync.dma_start(offs_sb[:], offs)
        load_scale_rows(w_s_raw[last_quadrant, :], w1_scales)
        load_scale_rows(w_s_raw[third_quadrant, 0:N], wd_scales)
        load_scale_rows(tab_s[last_quadrant, :], tab_scales)
        nc.sync.dma_start(pos1_sb[:], pos1)
        nc.sync.dma_start(pos2_sb[:], pos2)
        nc.sync.dma_start(out=tab_w[0][:], in_=tab_words[0].rearrange("p t i -> p (t i)").bitcast(I32))
        w1_by_group = w1_words.rearrange("a p (b c) -> b p a c", b=R_GROUPS)
        nc.sync.dma_start(out=w1_raw[0][:].bitcast(I32), in_=w1_by_group[0].bitcast(I32))
        nc.gpsimd.dma_start(out=least_sb[:], in_=least.rearrange("(b p i) -> p b i", b=R_GROUPS, i=PACK))
        nc.gpsimd.dma_start(out=base_sb[:], in_=base.rearrange("(p t) -> p t", t=PACK))
        nc.gpsimd.dma_start(out=gain_sb[:], in_=gain.rearrange("(p t) -> p t", t=PACK))

        deal(nc.vector.tensor_copy, w_s_rows[:], w_s_raw[:])
        spread_scale_rows(w1_s, w_s_rows[last_quadrant, :])
        tab_w.append(new("tab_w1", [P, T], I32, "w_s_raw"))
        nc.sync.dma_start(out=tab_w[1][:], in_=tab_words[1].rearrange("p t i -> p (t i)").bitcast(I32))
        nc.vector.tensor_copy(out=v_s_rows[:], in_=tab_s[:].indirect(offs_sb[:]))
        spread_scale_rows(v_s, v_s_rows[last_quadrant, :])
        w1_raw.append(new("w1_raw1", [P, K_GROUPS, 2 * GROUP], U8, "tab_s"))
        nc.sync.dma_start(out=w1_raw[1][:].bitcast(I32), in_=w1_by_group[1].bitcast(I32))

        for a in range(K_GROUPS):
            for lo, hi in HALVES:
                nc.vector.tensor_copy(out=v_w[a][:, lo:hi], in_=tab_w[a][:].bitcast(U32).indirect(entries(offs_sb, lo, hi)))

        for b in range(R_GROUPS):
            for a in range(K_GROUPS):
                deal(nc.scalar.copy, w1_w[a][b][:].bitcast(U16), w1_raw[b][:, a, :].bitcast(U16))

        wr_raw = [new("wr_raw0", [P, PACK, N], F32, "tab_w0")]
        nc.sync.dma_start(out=wr_raw[0][:], in_=wr[0:GROUP, :].rearrange("(p i) n -> p i n", i=PACK))
        wd_raw = new("wd_raw", [P, R_GROUPS, N], I32, "w1_raw0")
        nc.sync.dma_start(out=wd_raw[:], in_=wd_words.rearrange("b p c i -> p b (c i)").bitcast(I32))
        wd_s = new("wd_s", [P, R_GROUPS, N], U8, "v_s_all")
        nc.gpsimd.memset(wd_s[:].bitcast(I32), 0)
        spread_scale_rows(wd_s, w_s_rows[third_quadrant, 0:N])
        wr_raw.append(new("wr_raw1", [P, PACK, N], F32, "w_s_raw"))
        nc.sync.dma_start(out=wr_raw[1][:], in_=wr[GROUP : 2 * GROUP, :].rearrange("(p i) n -> p i n", i=PACK))

        def round_wr(b):
            nc.scalar.activation(
                out=wr_bf[b][:].rearrange("p (t m i) -> p m t i", t=PACK, i=PACK),
                in_=wr_raw[b][:].rearrange("p i (m t) -> p m t i", t=PACK),
                func=ACT.Copy,
            )

        def quantize(words, scales, src):
            nc.vector.quantize_mx(out=words.bitcast(FP8X4), scales=scales, in_=src)

        def first_stage_pass(bank, b, j0, a):
            cols = slice(j0, j0 + UNIT)
            for i in range(PACK):
                nc.tensor.matmul_mx(
                    out=bank[:, i, :],
                    lhsT=w1_w[a][b][:, 2 * P * i : 2 * P * (i + 1)].bitcast(FP4X4),
                    lhsT_scale=w1_s[:, a, GROUP * b + P * i : GROUP * b + P * (i + 1)],
                    rhs=v_w[a][:, cols].bitcast(FP8X4),
                    rhs_scale=v_s[:, a, cols],
                    start=(a == 0 and i == 0),
                    stop=(a == K_GROUPS - 1 and i == PACK - 1),
                )

        def open_bank(b, j0):
            bank = h_psum.tile([P, PACK, UNIT], F32, name="h_bank")
            first_stage_pass(bank, b, j0, 0)
            return bank

        def close_bank(bank, b, j0):
            first_stage_pass(bank, b, j0, 1)
            nc.vector.tensor_tensor(
                out=h_bf[b][:, PACK * j0 : PACK * (j0 + UNIT)].rearrange("p (j i) -> p j i", i=PACK),
                in0=bank[:].rearrange("p i j -> p j i"),
                in1=least_sb[:, b, :].unsqueeze(1).broadcast_to([P, UNIT, PACK]),
                op=ALU.max,
            )

        def first_stage(b, lo, hi):
            for j0 in range(lo, hi, UNIT):
                close_bank(open_bank(b, j0), b, j0)

        def quantize_h(b, lo, hi):
            quantize(h_w[b][:, lo:hi], h_s[b][:, lo:hi], h_bf[b][:, PACK * lo : PACK * hi])

        def quantize_wr(b):
            quantize(wr_w[b][:], wr_s[b][:], wr_bf[b][:])

        def scores(bank, c, t, words, scales):
            lo, hi = HALVES[c]
            for b in range(R_GROUPS):
                nc.tensor.matmul_mx(
                    out=bank[:],
                    lhsT=words[b][:, P * t : P * (t + 1)].bitcast(FP8X4),
                    lhsT_scale=scales[b][:, P * t : P * (t + 1)],
                    rhs=h_w[b][:, lo:hi].bitcast(FP8X4),
                    rhs_scale=h_s[b][:, lo:hi],
                    start=(b == 0),
                    stop=(b == R_GROUPS - 1),
                )

        def response(c, t):
            lo, hi = HALVES[c]
            bank = s_psum.tile([P, HALF], F32, name="s_bank")
            scores(bank, c, t, wr_w, wr_s)
            nc.vector.tensor_scalar(
                out=e_sb[t][:, lo:hi], in0=bank[:], scalar1=1.0, scalar2=(tops[t][c - 1][:] if c else None),
                op0=ALU.mult, op1=ALU.max, accum_out=tops[t][c][:],
            )

        def standby(c, t):
            lo, hi = HALVES[c]
            bank = h_psum.tile([P, HALF], F32, name="h_bank") if c else s_psum.tile([P, HALF], F32, name="s_bank")
            scores(bank, c, t, [wd_w[:, b, :] for b in range(R_GROUPS)], [wd_s[:, b, :] for b in range(R_GROUPS)])
            nc.scalar.copy(out=d_sb[t][:, lo:hi], in_=bank[:])

        round_wr(0)
        deal(nc.scalar.copy, wd_w[:].rearrange("p b c -> p (b c)"), wd_raw[:].rearrange("p b c -> p (b c)").bitcast(U32), "p g m i")
        round_wr(1)

        ahead = [(open_bank(0, j0), 0, j0) for j0 in range(0, BANKS_AHEAD * UNIT, UNIT)]
        for bank_and_place in ahead:
            close_bank(*bank_and_place)
        first_stage(0, BANKS_AHEAD * UNIT, HALF)
        first_stage(1, 0, UNIT)
        quantize_h(0, 0, HALF)
        first_stage(1, UNIT, HALF)
        first_stage(0, HALF, HALF + UNIT)
        quantize_h(1, 0, HALF)
        first_stage(0, HALF + UNIT, S)
        first_stage(1, HALF, HALF + UNIT)
        quantize_h(0, HALF, S)
        quantize_wr(0)
        first_stage(1, HALF + UNIT, S - UNIT)
        quantize_h(1, HALF, S - 2 * UNIT)
        quantize_wr(1)
        first_stage(1, S - UNIT, S)
        for t in range(PACK):
            standby(0, t)
        response(0, 0)
        quantize_h(1, S - 2 * UNIT, S)

        for t in range(PACK):
            if t + 1 < PACK:
                response(0, t + 1)
            response(1, t)
            nc.scalar.activation(out=neg_top[t][:], in_=tops[t][1][:], func=ACT.Copy, scale=-1.0)
            if t + 1 == PACK // 2:
                standby(1, 0)

        nc.gpsimd.tensor_tensor(out=gain_base[:], in0=gain_sb[:], in1=base_sb[:], op=ALU.mult)
        y_rows = out_0.rearrange("(p t) m -> p t m", t=PACK)
        for t in range(PACK):
            nc.scalar.activation(out=a_sb[t][:], in_=e_sb[t][:].indirect(pos1_sb[:]), func=ACT.Exp, bias=neg_top[t][:])
            if t > 0:
                standby(1, t)
            if t < LIFTS_ON_SCALAR:
                nc.scalar.activation(
                    out=lift[t][:], in_=a_sb[t][:], func=ACT.Identity,
                    scale=gain_sb[:, t : t + 1], bias=gain_base[:, t : t + 1],
                )
            else:
                nc.vector.tensor_scalar(
                    out=lift[t][:], in0=a_sb[t][:], scalar1=base_sb[:, t : t + 1], scalar2=gain_sb[:, t : t + 1],
                    op0=ALU.add, op1=ALU.mult,
                )
            for y_half, (lo, hi) in zip(y_sb, Y_HALVES):
                nc.vector.tensor_tensor(
                    out=y_half[:, t, :], in0=d_sb[t][:].indirect(entries(pos2_sb, lo, hi)), in1=lift[t][:, lo:hi], op=ALU.mult
                )
                nc.sync.dma_start(out=y_rows[:, t, lo:hi], in_=y_half[:, t, :])

        y_words = out_1[0].rearrange("p m t -> p (m t)").bitcast(I32)
        for copy, y_half, (lo, hi) in zip((nc.scalar.copy, nc.vector.tensor_copy), y_sb, Y_HALVES):
            copy(out=y_bf[:, PACK * lo : PACK * hi].rearrange("p (m t) -> p m t", t=PACK), in_=y_half[:].rearrange("p t m -> p m t"))
        for lo, hi in Y_HALVES:
            quantize(y_w[:, lo:hi], y_s[:, lo:hi], y_bf[:, PACK * lo : PACK * hi])
            nc.sync.dma_start(out=y_words[:, lo:hi], in_=y_w[:, lo:hi].bitcast(I32))
        for quad in range(QUADRANTS):
            engine = nc.scalar if quad % 2 else nc.sync
            engine.dma_start(out=out_2[0, 4 * quad : 4 * quad + 4, :].bitcast(I32), in_=y_s[32 * quad : 32 * quad + 4, :].bitcast(I32))
